import numpy as np
import ml_dtypes


def mxq(x, axis, fmt="e4m3"):
    dtype, down = {"e4m3": (ml_dtypes.float8_e4m3fn, 7), "e5m2": (ml_dtypes.float8_e5m2, 14)}[fmt]
    v = np.moveaxis(np.asarray(x, np.float32).astype(ml_dtypes.bfloat16).astype(np.float64), axis, -1)
    blocks = v.reshape(v.shape[:-1] + (-1, 32))
    amax = np.abs(blocks).max(-1, keepdims=True)
    byte = np.maximum(np.where(amax > 0, np.frexp(amax)[1] - 1 + 127, 0) - down, 1)
    scale = np.exp2(byte - 127.0)
    codes = (blocks / scale).astype(np.float32).astype(dtype).astype(np.float64)
    return np.moveaxis((codes * scale).reshape(v.shape), -1, axis)


WIDE = False


def mx_kscale(k):
    if not WIDE:
        return np.ones(k)
    levels = np.array([10, -10, 5, -5, 0])
    if k % 512:
        return np.exp2(np.random.permutation(np.resize(levels, k // 32))).repeat(32)
    a = np.empty((k // 512, 16))
    for p in range(k // 512):
        a[p, :8] = np.random.permutation(np.resize(levels, 8))
        for g in range(8):
            far = levels[np.abs(levels - a[p, g]) >= 10]
            a[p, g + 8] = far[np.random.randint(len(far))]
    return np.exp2(a.ravel()).repeat(32)


def f64(x):
    return np.asarray(x).astype(np.float64)


def striped(idx):
    return np.tile(idx.reshape(-1, 16).T, (8, 1)).astype(np.uint16)


def unstriped(offs):
    return offs[:16].T.reshape(-1).astype(np.int64)


def striped8(idx):
    return np.concatenate([x.reshape(-1, 16).T for x in idx]).astype(np.uint16)


def runs(offs, k):
    lists = np.stack([offs[16 * r : 16 * r + 16].T.reshape(-1) for r in range(8)]).astype(np.int64)
    return lists[np.arange(k) % 512 // 64]


def pack_weight(w):
    k, n = w.shape
    w = f64(np.asarray(w, np.float32).astype(ml_dtypes.bfloat16)).reshape(k // 32, 32, n)
    amax = np.abs(w).max(1)
    byte = np.clip(np.where(amax > 0, np.frexp(amax)[1] - 1 + 127 - 7, 1), 1, 254)
    scaled = (w * np.exp2(127.0 - byte)[:, None, :]).reshape(k, n).astype(np.float32)
    words = np.ascontiguousarray(scaled.reshape(k // 512, 128, 4, n).transpose(0, 1, 3, 2)).astype(ml_dtypes.float8_e4m3fn).view(np.uint8)
    return words, np.ascontiguousarray(byte.astype(np.uint8).reshape(k // 512, 16, n))


def unpack_weight(words, scales):
    g, p, n, _ = words.shape
    vals = np.ascontiguousarray(words).view(ml_dtypes.float8_e4m3fn).astype(np.float64) * np.repeat(np.exp2(scales.astype(np.float64) - 127.0), 8, axis=1)[..., None]
    return vals.transpose(0, 1, 3, 2).reshape(g * 512, n)

def planes(y):
    n, m = y.shape
    v = y.astype(np.float32).astype(ml_dtypes.bfloat16).astype(np.float64).reshape(n // 32, 32, m)
    top = np.abs(v).max(1)
    byte = np.clip(np.where(top > 0, np.frexp(top)[1] - 1 + 127 - 7, 1), 1, 254)
    codes = (v * np.exp2(127.0 - byte)[:, None, :]).reshape(n, m).astype(np.float32).astype(ml_dtypes.float8_e4m3fn).view(np.uint8)
    words = codes.reshape(n // 512, 128, 4, m).transpose(0, 1, 3, 2)
    return np.ascontiguousarray(words), np.ascontiguousarray(byte.astype(np.uint8).reshape(n // 512, 16, m))


K, T, S, N, H, W = 512, 2048, 512, 512, 512, 256


def setup_inputs():
    n = np.random.standard_normal
    s = mx_kscale(K)[:, None]
    u = mx_kscale(H)
    packed_xT = pack_weight(n((K, T)) * s)
    packed_w1 = pack_weight(n((K, H)) / np.sqrt(K) / s)
    packed_w2 = pack_weight(n((K, H)) / np.sqrt(K) / s)
    packed_w3 = pack_weight(n((H, N)) / np.sqrt(H) / u[:, None])
    return {
        "x_words": packed_xT[0],
        "x_scales": packed_xT[1],
        "w1_words": packed_w1[0],
        "w1_scales": packed_w1[1],
        "w2_words": packed_w2[0],
        "w2_scales": packed_w2[1],
        "gn": (np.random.uniform(0.5, 1.5, (H, 1)) * u[:, None]).astype(np.float32),
        "w3_words": packed_w3[0],
        "w3_scales": packed_w3[1],
        "offs": striped(np.random.permutation(T)[:S]),
        "two": striped(np.random.permutation(T)[:S]),
        "n1": striped8(np.stack([np.random.permutation(S)[:W] for _ in range(8)])),
        "n2": striped8(np.stack([np.random.permutation(S)[:W] for _ in range(8)])),
        "n3": striped8(np.stack([np.random.permutation(S) for _ in range(8)])),
        "n4": striped8(np.stack([np.random.permutation(S) for _ in range(8)])),
        "n5": striped8(np.stack([np.random.permutation(S) for _ in range(8)])),
    }


def reference(x_words, x_scales, w1_words, w1_scales, w2_words, w2_scales, gn, w3_words, w3_scales, offs, two, n1, n2, n3, n4, n5):
    x_two = unpack_weight(x_words, x_scales)[:, unstriped(two)]
    d = unpack_weight(w2_words, w2_scales).T @ x_two
    xq = unpack_weight(x_words, x_scales)[:, unstriped(offs)]
    y = unpack_weight(w1_words, w1_scales).T @ xq
    ra = d[np.arange(H)[:, None], runs(n2, H)] - (0.5 * (y[np.arange(H)[:, None], runs(n1, H)]))
    ds = y.copy()
    ds[np.arange(H)[:, None], runs(n1, H)] = ra
    z = f64(gn) * ds
    h = unpack_weight(w3_words, w3_scales).T @ mxq(z, 0, "e4m3")
    b1 = h[np.arange(N)[:, None], runs(n3, N)]
    b2 = h[np.arange(N)[:, None], runs(n4, N)]
    b3 = h[np.arange(N)[:, None], runs(n5, N)]
    out_0 = np.maximum(np.maximum(b1, b2), b3) - (0.5 * (np.maximum(np.minimum(b1, b2), np.minimum(np.maximum(b1, b2), b3))))
    return (out_0,) + planes(out_0)

@@ -1,0 +1,189 @@
+from contextlib import ExitStack
+
+import concourse.mybir as mybir
+
+K, T, S, N, H, W = 512, 2048, 512, 512, 512, 256
+FLOPS = 3 * 2 * 512 * 512 * 512
+
+F32 = mybir.dt.float32
+BF16 = mybir.dt.bfloat16
+I32 = mybir.dt.int32
+U32 = mybir.dt.uint32
+U16 = mybir.dt.uint16
+U8 = mybir.dt.uint8
+FP8X4 = mybir.dt.float8_e4m3fn_x4
+ALU = mybir.AluOpType
+ACT = mybir.ActivationFunctionType
+
+P = 128
+PACK = 4
+CHUNKS = (256, 128, 128)
+
+
+def tile_picked_twlputbtop2_none_po_kernel(
+    tc, x_words, x_scales, w1_words, w1_scales, w2_words, w2_scales, gn, w3_words, w3_scales,
+    offs, two, n1, n2, n3, n4, n5, out_0, out_1, out_2,
+):
+    nc = tc.nc
+    with ExitStack() as ctx:
+        held = ctx.enter_context(tc.tile_pool(name="held", bufs=1))
+        psum = ctx.enter_context(tc.psum_pool(name="psum", bufs=1))
+
+        def tile(name, shape, dtype):
+            return held.tile(shape, dtype, name=name, align_bytes=64)
+
+        def load_list(name, src):
+            t = tile(name, list(src.shape), U16)
+            nc.sync.dma_start(t[:], src)
+            return t
+
+        def load_words(name, src, width):
+            t = tile(name, [P, width], I32)
+            nc.sync.dma_start(t[:], src[0].rearrange("p n t -> p (n t)").bitcast(I32))
+            return t
+
+        def load_scale_rows(queue, dst, src, first):
+            for q in range(4):
+                queue.dma_start(
+                    dst[32 * q + first : 32 * q + first + 4, :].bitcast(I32),
+                    src[0, 4 * q : 4 * q + 4, :].bitcast(I32),
+                )
+
+        def deal(name, src, dtype):
+            t = tile(name, [P, H], dtype)
+            nc.vector.tensor_copy(
+                t[:].rearrange("p (t m) -> p m t", t=PACK),
+                src[:].rearrange("p (m t) -> p m t", t=PACK),
+            )
+            return t
+
+        x_sc = tile("x_sc", [P, T], U8)
+        w12_sc_raw = tile("w12_sc_raw", [P, H], U8)
+        w3_sc_raw = tile("w3_sc_raw", [P, N], U8)
+        nc.vector.memset(x_sc[:].bitcast(I32), 0)
+        nc.gpsimd.memset(w12_sc_raw[:].bitcast(I32), 0)
+        nc.gpsimd.memset(w3_sc_raw[:].bitcast(I32), 0)
+
+        offs_t = load_list("offs_t", offs)
+        two_t = load_list("two_t", two)
+        load_scale_rows(nc.scalar, x_sc, x_scales, 0)
+        x_w = load_words("x_w", x_words, T)
+        w1_raw = load_words("w1_raw", w1_words, H)
+        load_scale_rows(nc.scalar, w12_sc_raw, w1_scales, 0)
+        load_scale_rows(nc.gpsimd, w12_sc_raw, w2_scales, 4)
+        w2_raw = load_words("w2_raw", w2_words, H)
+        gain = tile("gain", [P, PACK], F32)
+        nc.sync.dma_start(gain[:], gn.rearrange("(p t) o -> p (t o)", t=PACK))
+        n1_t = load_list("n1_t", n1)
+        n2_t = load_list("n2_t", n2)
+        w3_raw = load_words("w3_raw", w3_words, N)
+        load_scale_rows(nc.gpsimd, w3_sc_raw, w3_scales, 0)
+        n3_t = load_list("n3_t", n3)
+        n4_t = load_list("n4_t", n4)
+        n5_t = load_list("n5_t", n5)
+
+        def pick_bytes(name, lst):
+            t = tile(name, [P, S], U8)
+            nc.vector.tensor_copy(t[:], x_sc[:].indirect(lst[:]))
+            return t
+
+        def pick_words(name, lst):
+            t = tile(name, [P, S], U32)
+            nc.vector.tensor_copy(t[:], x_w[:].bitcast(U32).indirect(lst[:]))
+            return t
+
+        def product(name, bank, w, w_sc, first, t, rhs, rhs_sc):
+            acc = psum.tile([P, S], F32, name=name + "_ps", tag="bank%d" % bank)
+            cols = slice(P * t, P * (t + 1))
+            nc.tensor.matmul_mx(
+                out=acc[:], lhsT=w[:, cols].bitcast(FP8X4), lhsT_scale=w_sc[first:P, cols],
+                rhs=rhs[:].bitcast(FP8X4), rhs_scale=rhs_sc[:], start=True, stop=True,
+            )
+            res = tile(name, [P, S], F32)
+            nc.scalar.copy(res[:], acc[:])
+            return res
+
+        xo_sc = pick_bytes("xo_sc", offs_t)
+        xt_sc = pick_bytes("xt_sc", two_t)
+        xo_w = pick_words("xo_w", offs_t)
+        w1 = deal("w1", w1_raw, I32)
+        w12_sc = deal("w12_sc", w12_sc_raw, U8)
+        xt_w = pick_words("xt_w", two_t)
+        w2 = deal("w2", w2_raw, I32)
+        w3 = deal("w3", w3_raw, I32)
+        w3_sc = deal("w3_sc", w3_sc_raw, U8)
+
+        half = S // 2
+        z_b = [tile("z_b%d" % a, [P, half, PACK], BF16) for a in range(2)]
+        for t in range(PACK):
+            y = product("y%d" % t, 2 * t, w1, w12_sc, 0, t, xo_w, xo_sc)
+            d = product("d%d" % t, 2 * t + 1, w2, w12_sc, 4, t, xt_w, xt_sc)
+            own = tile("own%d" % t, [P, W], F32)
+            other = tile("other%d" % t, [P, W], F32)
+            nc.vector.tensor_scalar(own[:], y[:].indirect(n1_t[:]), -0.5, 0.0, ALU.mult, ALU.add)
+            nc.vector.tensor_copy(other[:], d[:].indirect(n2_t[:]))
+            nc.vector.tensor_tensor(y[:].indirect(n1_t[:]), other[:], own[:], ALU.add)
+            nc.scalar.activation(z_b[0][:, :, t], y[:, :half], ACT.Copy, scale=gain[:, t : t + 1])
+            if t < 2:
+                nc.scalar.activation(z_b[1][:, :, t], y[:, half:], ACT.Copy, scale=gain[:, t : t + 1])
+            else:
+                nc.vector.tensor_scalar(z_b[1][:, :, t], y[:, half:], gain[:, t : t + 1], None, ALU.mult)
+
+        z_w = [tile("z_w%d" % a, [P, half], U32) for a in range(2)]
+        z_sc = [tile("z_sc%d" % a, [P, half], U8) for a in range(2)]
+        for a in (1, 0):
+            nc.vector.quantize_mx(
+                out=z_w[a][:].bitcast(FP8X4), scales=z_sc[a][:], in_=z_b[a][:].rearrange("p j t -> p (j t)")
+            )
+        h = [tile("h%d" % t, [P, S], F32) for t in range(PACK)]
+        for t in range(PACK):
+            for a in (1, 0):
+                acc = psum.tile([P, S], F32, name="h_ps%d_%d" % (t, a), tag="bank%d" % (2 * t + a))
+                cols = slice(P * t, P * (t + 1))
+                nc.tensor.matmul_mx(
+                    out=acc[:, :half], lhsT=w3[:, cols].bitcast(FP8X4), lhsT_scale=w3_sc[:, cols],
+                    rhs=z_w[a][:].bitcast(FP8X4), rhs_scale=z_sc[a][:], start=True, stop=True,
+                )
+                dst = h[t][:, a * half : (a + 1) * half]
+                if t == 0 and a == 0:
+                    nc.vector.tensor_copy(dst, acc[:, :half])
+                else:
+                    nc.scalar.copy(dst, acc[:, :half])
+
+        o_w = tile("o_w", [P, S], U32)
+        o_sc = tile("o_sc", [P, S], U8)
+        out_rows = out_0.rearrange("(p t) j -> p t j", t=PACK)
+        out_words = out_1[0].rearrange("p n t -> p (n t)").bitcast(I32)
+        c0 = 0
+        for c, width in enumerate(CHUNKS):
+            cols = slice(c0, c0 + width)
+            lst = slice(c0 // 16, (c0 + width) // 16)
+            b1, u, top, half_gap, w, low, best, res = [
+                tile("%s%d" % (name, c), [P, PACK, width], F32)
+                for name in ("b1_", "u_", "top_", "half_gap_", "w_", "low_", "best_", "res_")
+            ]
+            for t in range(PACK):
+                nc.vector.tensor_copy(b1[:, t, :], h[t][:].indirect(n3_t[:, lst]))
+                nc.vector.tensor_tensor(u[:, t, :], h[t][:].indirect(n4_t[:, lst]), b1[:, t, :], ALU.subtract)
+            nc.scalar.activation(half_gap[:], u[:], ACT.Abs, scale=0.5)
+            nc.vector.scalar_tensor_tensor(top[:], u[:], 0.0, b1[:], ALU.max, ALU.add)
+            for t in range(PACK):
+                nc.vector.tensor_tensor(w[:, t, :], h[t][:].indirect(n5_t[:, lst]), top[:, t, :], ALU.subtract)
+            nc.vector.scalar_tensor_tensor(low[:], w[:], -0.5, half_gap[:], ALU.mult, ALU.min)
+            nc.vector.tensor_tensor(best[:], w[:], low[:], ALU.max)
+            nc.vector.scalar_tensor_tensor(res[:], top[:], 0.5, best[:], ALU.mult, ALU.add)
+            nc.sync.dma_start(out_rows[:, :, cols], res[:])
+            res_b = tile("res_b%d" % c, [P, width, PACK], BF16)
+            nc.scalar.copy(
+                res_b[:].rearrange("p (c i) t -> p c t i", i=4),
+                res[:].rearrange("p t (c i) -> p c t i", i=4),
+            )
+            nc.vector.quantize_mx(
+                out=o_w[:, cols].bitcast(FP8X4), scales=o_sc[:, cols],
+                in_=res_b[:].rearrange("p j t -> p (j t)"),
+            )
+            nc.sync.dma_start(out_words[:, cols], o_w[:, cols].bitcast(I32))
+            c0 = c0 + width
+        for q in range(4):
+            queue = nc.scalar if q % 2 else nc.sync
+            queue.dma_start(out_2[0, 4 * q : 4 * q + 4, :].bitcast(I32), o_sc[32 * q : 32 * q + 4, :].bitcast(I32))

@@ -1,6 +1,7 @@
 from contextlib import ExitStack
 
 import concourse.mybir as mybir
+from concourse.masks import make_identity
 
 K, T, S, N, H, W = 512, 2048, 512, 512, 512, 256
 FLOPS = 3 * 2 * 512 * 512 * 512
@@ -17,7 +18,6 @@ ACT = mybir.ActivationFunctionType
 
 P = 128
 PACK = 4
-CHUNKS = (256, 128, 128)
 
 
 def tile_picked_twlputbtop2_none_po_kernel(
@@ -29,8 +29,8 @@ def tile_picked_twlputbtop2_none_po_kernel(
         held = ctx.enter_context(tc.tile_pool(name="held", bufs=1))
         psum = ctx.enter_context(tc.psum_pool(name="psum", bufs=1))
 
-        def tile(name, shape, dtype):
-            return held.tile(shape, dtype, name=name, align_bytes=64)
+        def tile(name, shape, dtype, tag=None):
+            return held.tile(shape, dtype, name=name, tag=tag or name, align_bytes=64)
 
         def load_list(name, src):
             t = tile(name, list(src.shape), U16)
@@ -58,29 +58,28 @@ def tile_picked_twlputbtop2_none_po_kernel(
             return t
 
         x_sc = tile("x_sc", [P, T], U8)
-        w12_sc_raw = tile("w12_sc_raw", [P, H], U8)
-        w3_sc_raw = tile("w3_sc_raw", [P, N], U8)
+        w1_sc_raw = tile("w1_sc_raw", [P, H], U8)
+        w23_sc_raw = tile("w23_sc_raw", [P, N], U8)
         nc.vector.memset(x_sc[:].bitcast(I32), 0)
-        nc.gpsimd.memset(w12_sc_raw[:].bitcast(I32), 0)
-        nc.gpsimd.memset(w3_sc_raw[:].bitcast(I32), 0)
+        nc.vector.memset(w1_sc_raw[:].bitcast(I32), 0)
+        nc.vector.memset(w23_sc_raw[:].bitcast(I32), 0)
 
+        x_w = load_words("x_w", x_words, T)
         offs_t = load_list("offs_t", offs)
         two_t = load_list("two_t", two)
-        load_scale_rows(nc.scalar, x_sc, x_scales, 0)
-        x_w = load_words("x_w", x_words, T)
-        w1_raw = load_words("w1_raw", w1_words, H)
-        load_scale_rows(nc.scalar, w12_sc_raw, w1_scales, 0)
-        load_scale_rows(nc.gpsimd, w12_sc_raw, w2_scales, 4)
-        w2_raw = load_words("w2_raw", w2_words, H)
-        gain = tile("gain", [P, PACK], F32)
-        nc.sync.dma_start(gain[:], gn.rearrange("(p t) o -> p (t o)", t=PACK))
         n1_t = load_list("n1_t", n1)
         n2_t = load_list("n2_t", n2)
-        w3_raw = load_words("w3_raw", w3_words, N)
-        load_scale_rows(nc.gpsimd, w3_sc_raw, w3_scales, 0)
         n3_t = load_list("n3_t", n3)
         n4_t = load_list("n4_t", n4)
         n5_t = load_list("n5_t", n5)
+        load_scale_rows(nc.scalar, x_sc, x_scales, 0)
+        w1_raw = load_words("w13_raw", w1_words, H)
+        load_scale_rows(nc.scalar, w1_sc_raw, w1_scales, 0)
+        w2_raw = load_words("w2_raw", w2_words, H)
+        load_scale_rows(nc.scalar, w23_sc_raw, w2_scales, 0)
+        load_scale_rows(nc.gpsimd, w23_sc_raw, w3_scales, 4)
+        gain = tile("gain", [P, PACK], F32)
+        nc.gpsimd.dma_start(gain[:], gn.rearrange("(p t) o -> p (t o)", t=PACK))
 
         def pick_bytes(name, lst):
             t = tile(name, [P, S], U8)
@@ -103,26 +102,29 @@ def tile_picked_twlputbtop2_none_po_kernel(
             nc.scalar.copy(res[:], acc[:])
             return res
 
-        xo_sc = pick_bytes("xo_sc", offs_t)
-        xt_sc = pick_bytes("xt_sc", two_t)
+        ident = tile("ident", [P, P], F32)
+        make_identity(nc, ident[:])
         xo_w = pick_words("xo_w", offs_t)
-        w1 = deal("w1", w1_raw, I32)
-        w12_sc = deal("w12_sc", w12_sc_raw, U8)
         xt_w = pick_words("xt_w", two_t)
+        xo_sc = pick_bytes("xo_sc", offs_t)
+        w1 = deal("w1", w1_raw, I32)
+        w1_sc = deal("w1_sc", w1_sc_raw, U8)
+        w3_raw = load_words("w13_raw", w3_words, N)
+        xt_sc = pick_bytes("xt_sc", two_t)
         w2 = deal("w2", w2_raw, I32)
+        w23_sc = deal("w23_sc", w23_sc_raw, U8)
         w3 = deal("w3", w3_raw, I32)
-        w3_sc = deal("w3_sc", w3_sc_raw, U8)
 
+        own = tile("own", [P, PACK, W], F32, "w23_sc_raw")
         half = S // 2
         z_b = [tile("z_b%d" % a, [P, half, PACK], BF16) for a in range(2)]
         for t in range(PACK):
-            y = product("y%d" % t, 2 * t, w1, w12_sc, 0, t, xo_w, xo_sc)
-            d = product("d%d" % t, 2 * t + 1, w2, w12_sc, 4, t, xt_w, xt_sc)
-            own = tile("own%d" % t, [P, W], F32)
+            y = product("y%d" % t, 2 * t, w1, w1_sc, 0, t, xo_w, xo_sc)
+            d = product("d%d" % t, 2 * t + 1, w2, w23_sc, 0, t, xt_w, xt_sc)
             other = tile("other%d" % t, [P, W], F32)
-            nc.vector.tensor_scalar(own[:], y[:].indirect(n1_t[:]), -0.5, 0.0, ALU.mult, ALU.add)
+            nc.vector.tensor_scalar(own[:, t, :], y[:].indirect(n1_t[:]), -0.5, 0.0, ALU.mult, ALU.add)
             nc.vector.tensor_copy(other[:], d[:].indirect(n2_t[:]))
-            nc.vector.tensor_tensor(y[:].indirect(n1_t[:]), other[:], own[:], ALU.add)
+            nc.vector.tensor_tensor(y[:].indirect(n1_t[:]), other[:], own[:, t, :], ALU.add)
             nc.scalar.activation(z_b[0][:, :, t], y[:, :half], ACT.Copy, scale=gain[:, t : t + 1])
             if t < 2:
                 nc.scalar.activation(z_b[1][:, :, t], y[:, half:], ACT.Copy, scale=gain[:, t : t + 1])
@@ -141,7 +143,7 @@ def tile_picked_twlputbtop2_none_po_kernel(
                 acc = psum.tile([P, S], F32, name="h_ps%d_%d" % (t, a), tag="bank%d" % (2 * t + a))
                 cols = slice(P * t, P * (t + 1))
                 nc.tensor.matmul_mx(
-                    out=acc[:, :half], lhsT=w3[:, cols].bitcast(FP8X4), lhsT_scale=w3_sc[:, cols],
+                    out=acc[:, :half], lhsT=w3[:, cols].bitcast(FP8X4), lhsT_scale=w23_sc[4:P, cols],
                     rhs=z_w[a][:].bitcast(FP8X4), rhs_scale=z_sc[a][:], start=True, stop=True,
                 )
                 dst = h[t][:, a * half : (a + 1) * half]
@@ -154,36 +156,72 @@ def tile_picked_twlputbtop2_none_po_kernel(
         o_sc = tile("o_sc", [P, S], U8)
         out_rows = out_0.rearrange("(p t) j -> p t j", t=PACK)
         out_words = out_1[0].rearrange("p n t -> p (n t)").bitcast(I32)
-        c0 = 0
-        for c, width in enumerate(CHUNKS):
-            cols = slice(c0, c0 + width)
-            lst = slice(c0 // 16, (c0 + width) // 16)
-            b1, u, top, half_gap, w, low, best, res = [
-                tile("%s%d" % (name, c), [P, PACK, width], F32)
-                for name in ("b1_", "u_", "top_", "half_gap_", "w_", "low_", "best_", "res_")
-            ]
+        banks = []
+
+        def bank(name):
+            banks.append(name)
+            return psum.tile([P, PACK, P], F32, name=name, tag="bank%d" % ((len(banks) - 1) % 8))
+
+        def turned_sum(name, terms):
+            acc = bank(name)
             for t in range(PACK):
-                nc.vector.tensor_copy(b1[:, t, :], h[t][:].indirect(n3_t[:, lst]))
-                nc.vector.tensor_tensor(u[:, t, :], h[t][:].indirect(n4_t[:, lst]), b1[:, t, :], ALU.subtract)
-            nc.scalar.activation(half_gap[:], u[:], ACT.Abs, scale=0.5)
-            nc.vector.scalar_tensor_tensor(top[:], u[:], 0.0, b1[:], ALU.max, ALU.add)
-            for t in range(PACK):
-                nc.vector.tensor_tensor(w[:, t, :], h[t][:].indirect(n5_t[:, lst]), top[:, t, :], ALU.subtract)
-            nc.vector.scalar_tensor_tensor(low[:], w[:], -0.5, half_gap[:], ALU.mult, ALU.min)
-            nc.vector.tensor_tensor(best[:], w[:], low[:], ALU.max)
-            nc.vector.scalar_tensor_tensor(res[:], top[:], 0.5, best[:], ALU.mult, ALU.add)
-            nc.sync.dma_start(out_rows[:, :, cols], res[:])
-            res_b = tile("res_b%d" % c, [P, width, PACK], BF16)
-            nc.scalar.copy(
+                for i, term in enumerate(terms):
+                    nc.tensor.matmul(
+                        acc[:, t, :], lhsT=term[:, t, :], rhs=ident[:], is_transpose=True,
+                        start=(i == 0), stop=(i == len(terms) - 1),
+                    )
+            return acc
+
+        def hand_out(name, res, cols, width, engine):
+            nc.sync.dma_start(out_rows[:, :, cols], res)
+            res_b = tile(name, [P, width, PACK], BF16)
+            engine(
                 res_b[:].rearrange("p (c i) t -> p c t i", i=4),
-                res[:].rearrange("p t (c i) -> p c t i", i=4),
+                res.rearrange("p t (c i) -> p c t i", i=4),
             )
             nc.vector.quantize_mx(
                 out=o_w[:, cols].bitcast(FP8X4), scales=o_sc[:, cols],
                 in_=res_b[:].rearrange("p j t -> p (j t)"),
             )
             nc.sync.dma_start(out_words[:, cols], o_w[:, cols].bitcast(I32))
-            c0 = c0 + width
+
+        def fetch(c, c0, width, b1_tag):
+            lst = slice(c0 // 16, (c0 + width) // 16)
+            b1 = tile("b1_%d" % c, [P, PACK, width], F32, b1_tag)
+            u = tile("u_%d" % c, [P, PACK, width], F32, "u")
+            top, w = [tile("%s%d" % (name, c), [P, PACK, width], F32) for name in ("top_", "w_")]
+            for t in range(PACK):
+                nc.vector.tensor_copy(b1[:, t, :], h[t][:].indirect(n3_t[:, lst]))
+                nc.vector.tensor_tensor(u[:, t, :], h[t][:].indirect(n4_t[:, lst]), b1[:, t, :], ALU.subtract)
+            nc.vector.scalar_tensor_tensor(top[:], u[:], 0.0, b1[:], ALU.max, ALU.add)
+            for t in range(PACK):
+                nc.vector.tensor_tensor(w[:, t, :], h[t][:].indirect(n5_t[:, lst]), top[:, t, :], ALU.subtract)
+            return u, top, w
+
+        def block(name, tag=None):
+            return tile(name, [P, PACK, P], F32, tag)
+
+        for i in range(3):
+            u, top, w = fetch(i, P * i, P, "b1_%d" % (i % 2))
+            gap, over = block("gap%d" % i, "gap"), block("over%d" % i, "over")
+            cut, lin, res = block("cut%d" % i), block("lin%d" % i), block("res%d" % i)
+            nc.scalar.activation(gap[:], u[:], ACT.Abs)
+            nc.scalar.activation(over[:], w[:], ACT.Relu, scale=3.0)
+            acc = turned_sum("r%d" % i, [gap[:], w[:]])
+            nc.scalar.activation(cut[:], acc[:], ACT.Relu)
+            acc = turned_sum("s%d" % i, [top[:], gap[:], over[:]])
+            nc.scalar.activation(lin[:], acc[:], ACT.Copy, scale=-1.0)
+            acc = turned_sum("b%d" % i, [cut[:], lin[:]])
+            nc.scalar.activation(res[:], acc[:], ACT.Copy, scale=-0.5)
+            hand_out("res_b%d" % i, res[:], slice(P * i, P * (i + 1)), P, nc.scalar.copy)
+
+        u, top, w = fetch(3, 3 * P, P, "b1_1")
+        gap, low, best, res = block("gap3", "gap"), block("low3"), block("best3"), block("res3")
+        nc.scalar.activation(gap[:], u[:], ACT.Abs, scale=0.5)
+        nc.vector.scalar_tensor_tensor(low[:], w[:], -0.5, gap[:], ALU.mult, ALU.min)
+        nc.vector.tensor_tensor(best[:], w[:], low[:], ALU.max)
+        nc.vector.scalar_tensor_tensor(res[:], top[:], 0.5, best[:], ALU.mult, ALU.add)
+        hand_out("res_b3", res[:], slice(3 * P, 4 * P), P, nc.vector.tensor_copy)
         for q in range(4):
             queue = nc.scalar if q % 2 else nc.sync
             queue.dma_start(out_2[0, 4 * q : 4 * q + 4, :].bitcast(I32), o_sc[32 * q : 32 * q + 4, :].bitcast(I32))

@@ -192,8 +192,10 @@ def tile_picked_twlputbtop2_none_po_kernel(
             top, w = [tile("%s%d" % (name, c), [P, PACK, width], F32) for name in ("top_", "w_")]
             for t in range(PACK):
                 nc.vector.tensor_copy(b1[:, t, :], h[t][:].indirect(n3_t[:, lst]))
+            for t in range(PACK):
                 nc.vector.tensor_tensor(u[:, t, :], h[t][:].indirect(n4_t[:, lst]), b1[:, t, :], ALU.subtract)
-            nc.vector.scalar_tensor_tensor(top[:], u[:], 0.0, b1[:], ALU.max, ALU.add)
+            for ts in (slice(0, 2), slice(2, 4)):
+                nc.vector.scalar_tensor_tensor(top[:, ts, :], u[:, ts, :], 0.0, b1[:, ts, :], ALU.max, ALU.add)
             for t in range(PACK):
                 nc.vector.tensor_tensor(w[:, t, :], h[t][:].indirect(n5_t[:, lst]), top[:, t, :], ALU.subtract)
             return u, top, w
@@ -202,25 +204,35 @@ def tile_picked_twlputbtop2_none_po_kernel(
             return tile(name, [P, PACK, P], F32, tag)
 
         for i in range(3):
-            u, top, w = fetch(i, P * i, P, "b1_%d" % (i % 2))
+            u, top, w = fetch(i, P * i, P, "b1")
             gap, over = block("gap%d" % i, "gap"), block("over%d" % i, "over")
-            cut, lin, res = block("cut%d" % i), block("lin%d" % i), block("res%d" % i)
+            lin, res = block("lin%d" % i), block("res%d" % i)
             nc.scalar.activation(gap[:], u[:], ACT.Abs)
             nc.scalar.activation(over[:], w[:], ACT.Relu, scale=3.0)
-            acc = turned_sum("r%d" % i, [gap[:], w[:]])
-            nc.scalar.activation(cut[:], acc[:], ACT.Relu)
-            acc = turned_sum("s%d" % i, [top[:], gap[:], over[:]])
-            nc.scalar.activation(lin[:], acc[:], ACT.Copy, scale=-1.0)
-            acc = turned_sum("b%d" % i, [cut[:], lin[:]])
-            nc.scalar.activation(res[:], acc[:], ACT.Copy, scale=-0.5)
+            if i < 2:
+                cut = block("cut%d" % i)
+                acc = turned_sum("r%d" % i, [gap[:], w[:]])
+                nc.scalar.activation(cut[:], acc[:], ACT.Relu)
+                acc = turned_sum("s%d" % i, [top[:], gap[:], over[:]])
+                nc.scalar.activation(lin[:], acc[:], ACT.Copy, scale=-1.0)
+                acc = turned_sum("b%d" % i, [cut[:], lin[:]])
+                nc.scalar.activation(res[:], acc[:], ACT.Copy, scale=-0.5)
+            else:
+                low = block("low%d" % i)
+                nc.vector.scalar_tensor_tensor(low[:], w[:], -1.0, gap[:], ALU.mult, ALU.min)
+                acc = turned_sum("s%d" % i, [top[:], over[:], low[:]])
+                nc.scalar.copy(lin[:], acc[:])
+                acc = turned_sum("b%d" % i, [lin[:]])
+                nc.scalar.activation(res[:], acc[:], ACT.Copy, scale=0.5)
             hand_out("res_b%d" % i, res[:], slice(P * i, P * (i + 1)), P, nc.scalar.copy)
 
-        u, top, w = fetch(3, 3 * P, P, "b1_1")
-        gap, low, best, res = block("gap3", "gap"), block("low3"), block("best3"), block("res3")
+        u, top, w = fetch(3, 3 * P, P, "b1")
+        gap, low, best, res = block("gap3", "over"), block("low3"), block("best3"), block("res3")
         nc.scalar.activation(gap[:], u[:], ACT.Abs, scale=0.5)
-        nc.vector.scalar_tensor_tensor(low[:], w[:], -0.5, gap[:], ALU.mult, ALU.min)
-        nc.vector.tensor_tensor(best[:], w[:], low[:], ALU.max)
-        nc.vector.scalar_tensor_tensor(res[:], top[:], 0.5, best[:], ALU.mult, ALU.add)
+        for ts in (slice(0, 2), slice(2, 4)):
+            nc.vector.scalar_tensor_tensor(low[:, ts, :], w[:, ts, :], -0.5, gap[:, ts, :], ALU.mult, ALU.min)
+            nc.vector.tensor_tensor(best[:, ts, :], w[:, ts, :], low[:, ts, :], ALU.max)
+            nc.vector.scalar_tensor_tensor(res[:, ts, :], top[:, ts, :], 0.5, best[:, ts, :], ALU.mult, ALU.add)
         hand_out("res_b3", res[:], slice(3 * P, 4 * P), P, nc.vector.tensor_copy)
         for q in range(4):
             queue = nc.scalar if q % 2 else nc.sync

from contextlib import ExitStack

import concourse.mybir as mybir
from concourse.masks import make_identity

K, T, S, N, H, W = 512, 2048, 512, 512, 512, 256
FLOPS = 3 * 2 * 512 * 512 * 512

F32 = mybir.dt.float32
BF16 = mybir.dt.bfloat16
I32 = mybir.dt.int32
U32 = mybir.dt.uint32
U16 = mybir.dt.uint16
U8 = mybir.dt.uint8
FP8X4 = mybir.dt.float8_e4m3fn_x4
ALU = mybir.AluOpType
ACT = mybir.ActivationFunctionType

P = 128
PACK = 4


def tile_picked_twlputbtop2_none_po_kernel(
    tc, x_words, x_scales, w1_words, w1_scales, w2_words, w2_scales, gn, w3_words, w3_scales,
    offs, two, n1, n2, n3, n4, n5, out_0, out_1, out_2,
):
    nc = tc.nc
    with ExitStack() as ctx:
        held = ctx.enter_context(tc.tile_pool(name="held", bufs=1))
        psum = ctx.enter_context(tc.psum_pool(name="psum", bufs=1))

        def tile(name, shape, dtype, tag=None):
            return held.tile(shape, dtype, name=name, tag=tag or name, align_bytes=64)

        def load_list(name, src):
            t = tile(name, list(src.shape), U16)
            nc.sync.dma_start(t[:], src)
            return t

        def load_words(name, src, width):
            t = tile(name, [P, width], I32)
            nc.sync.dma_start(t[:], src[0].rearrange("p n t -> p (n t)").bitcast(I32))
            return t

        def load_scale_rows(queue, dst, src, first):
            for q in range(4):
                queue.dma_start(
                    dst[32 * q + first : 32 * q + first + 4, :].bitcast(I32),
                    src[0, 4 * q : 4 * q + 4, :].bitcast(I32),
                )

        def deal(name, src, dtype):
            t = tile(name, [P, H], dtype)
            nc.vector.tensor_copy(
                t[:].rearrange("p (t m) -> p m t", t=PACK),
                src[:].rearrange("p (m t) -> p m t", t=PACK),
            )
            return t

        x_sc = tile("x_sc", [P, T], U8)
        w1_sc_raw = tile("w1_sc_raw", [P, H], U8)
        w23_sc_raw = tile("w23_sc_raw", [P, N], U8)
        nc.vector.memset(x_sc[:].bitcast(I32), 0)
        nc.vector.memset(w1_sc_raw[:].bitcast(I32), 0)
        nc.vector.memset(w23_sc_raw[:].bitcast(I32), 0)

        x_w = load_words("x_w", x_words, T)
        offs_t = load_list("offs_t", offs)
        two_t = load_list("two_t", two)
        n1_t = load_list("n1_t", n1)
        n2_t = load_list("n2_t", n2)
        n3_t = load_list("n3_t", n3)
        n4_t = load_list("n4_t", n4)
        n5_t = load_list("n5_t", n5)
        load_scale_rows(nc.scalar, x_sc, x_scales, 0)
        w1_raw = load_words("w13_raw", w1_words, H)
        load_scale_rows(nc.scalar, w1_sc_raw, w1_scales, 0)
        w2_raw = load_words("w2_raw", w2_words, H)
        load_scale_rows(nc.scalar, w23_sc_raw, w2_scales, 0)
        load_scale_rows(nc.gpsimd, w23_sc_raw, w3_scales, 4)
        gain = tile("gain", [P, PACK], F32)
        nc.gpsimd.dma_start(gain[:], gn.rearrange("(p t) o -> p (t o)", t=PACK))

        def pick_bytes(name, lst):
            t = tile(name, [P, S], U8)
            nc.vector.tensor_copy(t[:], x_sc[:].indirect(lst[:]))
            return t

        def pick_words(name, lst):
            t = tile(name, [P, S], U32)
            nc.vector.tensor_copy(t[:], x_w[:].bitcast(U32).indirect(lst[:]))
            return t

        def product(name, bank, w, w_sc, first, t, rhs, rhs_sc):
            acc = psum.tile([P, S], F32, name=name + "_ps", tag="bank%d" % bank)
            cols = slice(P * t, P * (t + 1))
            nc.tensor.matmul_mx(
                out=acc[:], lhsT=w[:, cols].bitcast(FP8X4), lhsT_scale=w_sc[first:P, cols],
                rhs=rhs[:].bitcast(FP8X4), rhs_scale=rhs_sc[:], start=True, stop=True,
            )
            res = tile(name, [P, S], F32)
            nc.scalar.copy(res[:], acc[:])
            return res

        ident = tile("ident", [P, P], F32)
        make_identity(nc, ident[:])
        xo_w = pick_words("xo_w", offs_t)
        xt_w = pick_words("xt_w", two_t)
        xo_sc = pick_bytes("xo_sc", offs_t)
        w1 = deal("w1", w1_raw, I32)
        w1_sc = deal("w1_sc", w1_sc_raw, U8)
        w3_raw = load_words("w13_raw", w3_words, N)
        xt_sc = pick_bytes("xt_sc", two_t)
        w2 = deal("w2", w2_raw, I32)
        w23_sc = deal("w23_sc", w23_sc_raw, U8)
        w3 = deal("w3", w3_raw, I32)

        own = tile("own", [P, PACK, W], F32, "w23_sc_raw")
        half = S // 2
        z_b = [tile("z_b%d" % a, [P, half, PACK], BF16) for a in range(2)]
        for t in range(PACK):
            y = product("y%d" % t, 2 * t, w1, w1_sc, 0, t, xo_w, xo_sc)
            d = product("d%d" % t, 2 * t + 1, w2, w23_sc, 0, t, xt_w, xt_sc)
            other = tile("other%d" % t, [P, W], F32)
            nc.vector.tensor_scalar(own[:, t, :], y[:].indirect(n1_t[:]), -0.5, 0.0, ALU.mult, ALU.add)
            nc.vector.tensor_copy(other[:], d[:].indirect(n2_t[:]))
            nc.vector.tensor_tensor(y[:].indirect(n1_t[:]), other[:], own[:, t, :], ALU.add)
            nc.scalar.activation(z_b[0][:, :, t], y[:, :half], ACT.Copy, scale=gain[:, t : t + 1])
            if t < 2:
                nc.scalar.activation(z_b[1][:, :, t], y[:, half:], ACT.Copy, scale=gain[:, t : t + 1])
            else:
                nc.vector.tensor_scalar(z_b[1][:, :, t], y[:, half:], gain[:, t : t + 1], None, ALU.mult)

        z_w = [tile("z_w%d" % a, [P, half], U32) for a in range(2)]
        z_sc = [tile("z_sc%d" % a, [P, half], U8) for a in range(2)]
        for a in (1, 0):
            nc.vector.quantize_mx(
                out=z_w[a][:].bitcast(FP8X4), scales=z_sc[a][:], in_=z_b[a][:].rearrange("p j t -> p (j t)")
            )
        h = [tile("h%d" % t, [P, S], F32) for t in range(PACK)]
        for t in range(PACK):
            for a in (1, 0):
                acc = psum.tile([P, S], F32, name="h_ps%d_%d" % (t, a), tag="bank%d" % (2 * t + a))
                cols = slice(P * t, P * (t + 1))
                nc.tensor.matmul_mx(
                    out=acc[:, :half], lhsT=w3[:, cols].bitcast(FP8X4), lhsT_scale=w23_sc[4:P, cols],
                    rhs=z_w[a][:].bitcast(FP8X4), rhs_scale=z_sc[a][:], start=True, stop=True,
                )
                dst = h[t][:, a * half : (a + 1) * half]
                if t == 0 and a == 0:
                    nc.vector.tensor_copy(dst, acc[:, :half])
                else:
                    nc.scalar.copy(dst, acc[:, :half])

        o_w = tile("o_w", [P, S], U32)
        o_sc = tile("o_sc", [P, S], U8)
        out_rows = out_0.rearrange("(p t) j -> p t j", t=PACK)
        out_words = out_1[0].rearrange("p n t -> p (n t)").bitcast(I32)
        banks = []

        def bank(name):
            banks.append(name)
            return psum.tile([P, PACK, P], F32, name=name, tag="bank%d" % ((len(banks) - 1) % 8))

        def turned_sum(name, terms):
            acc = bank(name)
            for t in range(PACK):
                for i, term in enumerate(terms):
                    nc.tensor.matmul(
                        acc[:, t, :], lhsT=term[:, t, :], rhs=ident[:], is_transpose=True,
                        start=(i == 0), stop=(i == len(terms) - 1),
                    )
            return acc

        def hand_out(name, res, cols, width, engine):
            nc.sync.dma_start(out_rows[:, :, cols], res)
            res_b = tile(name, [P, width, PACK], BF16)
            engine(
                res_b[:].rearrange("p (c i) t -> p c t i", i=4),
                res.rearrange("p t (c i) -> p c t i", i=4),
            )
            nc.vector.quantize_mx(
                out=o_w[:, cols].bitcast(FP8X4), scales=o_sc[:, cols],
                in_=res_b[:].rearrange("p j t -> p (j t)"),
            )
            nc.sync.dma_start(out_words[:, cols], o_w[:, cols].bitcast(I32))

        def fetch(c, c0, width, b1_tag):
            lst = slice(c0 // 16, (c0 + width) // 16)
            b1 = tile("b1_%d" % c, [P, PACK, width], F32, b1_tag)
            u = tile("u_%d" % c, [P, PACK, width], F32, "u")
            top, w = [tile("%s%d" % (name, c), [P, PACK, width], F32) for name in ("top_", "w_")]
            for t in range(PACK):
                nc.vector.tensor_copy(b1[:, t, :], h[t][:].indirect(n3_t[:, lst]))
            for t in range(PACK):
                nc.vector.tensor_tensor(u[:, t, :], h[t][:].indirect(n4_t[:, lst]), b1[:, t, :], ALU.subtract)
            for ts in (slice(0, 2), slice(2, 4)):
                nc.vector.scalar_tensor_tensor(top[:, ts, :], u[:, ts, :], 0.0, b1[:, ts, :], ALU.max, ALU.add)
            for t in range(PACK):
                nc.vector.tensor_tensor(w[:, t, :], h[t][:].indirect(n5_t[:, lst]), top[:, t, :], ALU.subtract)
            return u, top, w

        def block(name, tag=None):
            return tile(name, [P, PACK, P], F32, tag)

        for i in range(3):
            u, top, w = fetch(i, P * i, P, "b1")
            gap, over = block("gap%d" % i, "gap"), block("over%d" % i, "over")
            lin, res = block("lin%d" % i), block("res%d" % i)
            nc.scalar.activation(gap[:], u[:], ACT.Abs)
            nc.scalar.activation(over[:], w[:], ACT.Relu, scale=3.0)
            if i < 2:
                cut = block("cut%d" % i)
                acc = turned_sum("r%d" % i, [gap[:], w[:]])
                nc.scalar.activation(cut[:], acc[:], ACT.Relu)
                acc = turned_sum("s%d" % i, [top[:], gap[:], over[:]])
                nc.scalar.activation(lin[:], acc[:], ACT.Copy, scale=-1.0)
                acc = turned_sum("b%d" % i, [cut[:], lin[:]])
                nc.scalar.activation(res[:], acc[:], ACT.Copy, scale=-0.5)
            else:
                low = block("low%d" % i)
                nc.vector.scalar_tensor_tensor(low[:], w[:], -1.0, gap[:], ALU.mult, ALU.min)
                acc = turned_sum("s%d" % i, [top[:], over[:], low[:]])
                nc.scalar.copy(lin[:], acc[:])
                acc = turned_sum("b%d" % i, [lin[:]])
                nc.scalar.activation(res[:], acc[:], ACT.Copy, scale=0.5)
            hand_out("res_b%d" % i, res[:], slice(P * i, P * (i + 1)), P, nc.scalar.copy)

        u, top, w = fetch(3, 3 * P, P, "b1")
        gap, low, best, res = block("gap3", "over"), block("low3"), block("best3"), block("res3")
        nc.scalar.activation(gap[:], u[:], ACT.Abs, scale=0.5)
        for ts in (slice(0, 2), slice(2, 4)):
            nc.vector.scalar_tensor_tensor(low[:, ts, :], w[:, ts, :], -0.5, gap[:, ts, :], ALU.mult, ALU.min)
            nc.vector.tensor_tensor(best[:, ts, :], w[:, ts, :], low[:, ts, :], ALU.max)
            nc.vector.scalar_tensor_tensor(res[:, ts, :], top[:, ts, :], 0.5, best[:, ts, :], ALU.mult, ALU.add)
        hand_out("res_b3", res[:], slice(3 * P, 4 * P), P, nc.vector.tensor_copy)
        for q in range(4):
            queue = nc.scalar if q % 2 else nc.sync
            queue.dma_start(out_2[0, 4 * q : 4 * q + 4, :].bitcast(I32), o_sc[32 * q : 32 * q + 4, :].bitcast(I32))
